import numpy as np
import ml_dtypes


def mxq(x, axis, fmt="e4m3"):
    dtype, down = {"e4m3": (ml_dtypes.float8_e4m3fn, 7), "e5m2": (ml_dtypes.float8_e5m2, 14)}[fmt]
    v = np.moveaxis(np.asarray(x, np.float32).astype(ml_dtypes.bfloat16).astype(np.float64), axis, -1)
    blocks = v.reshape(v.shape[:-1] + (-1, 32))
    amax = np.abs(blocks).max(-1, keepdims=True)
    byte = np.maximum(np.where(amax > 0, np.frexp(amax)[1] - 1 + 127, 0) - down, 1)
    scale = np.exp2(byte - 127.0)
    codes = (blocks / scale).astype(np.float32).astype(dtype).astype(np.float64)
    return np.moveaxis((codes * scale).reshape(v.shape), -1, axis)


WIDE = False


def mx_kscale(k):
    if not WIDE:
        return np.ones(k)
    levels = np.array([10, -10, 5, -5, 0])
    if k % 512:
        return np.exp2(np.random.permutation(np.resize(levels, k // 32))).repeat(32)
    a = np.empty((k // 512, 16))
    for p in range(k // 512):
        a[p, :8] = np.random.permutation(np.resize(levels, 8))
        for g in range(8):
            far = levels[np.abs(levels - a[p, g]) >= 10]
            a[p, g + 8] = far[np.random.randint(len(far))]
    return np.exp2(a.ravel()).repeat(32)


def f64(x):
    return np.asarray(x).astype(np.float64)


def striped(idx):
    return np.tile(idx.reshape(-1, 16).T, (8, 1)).astype(np.uint16)


def unstriped(offs):
    return offs[:16].T.reshape(-1).astype(np.int64)


def pack_weight(w):
    k, n = w.shape
    w = f64(np.asarray(w, np.float32).astype(ml_dtypes.bfloat16)).reshape(k // 32, 32, n)
    amax = np.abs(w).max(1)
    byte = np.clip(np.where(amax > 0, np.frexp(amax)[1] - 1 + 127 - 7, 1), 1, 254)
    scaled = (w * np.exp2(127.0 - byte)[:, None, :]).reshape(k, n).astype(np.float32)
    words = np.ascontiguousarray(scaled.reshape(k // 512, 128, 4, n).transpose(0, 1, 3, 2)).astype(ml_dtypes.float8_e4m3fn).view(np.uint8)
    return words, np.ascontiguousarray(byte.astype(np.uint8).reshape(k // 512, 16, n))


def unpack_weight(words, scales):
    g, p, n, _ = words.shape
    vals = np.ascontiguousarray(words).view(ml_dtypes.float8_e4m3fn).astype(np.float64) * np.repeat(np.exp2(scales.astype(np.float64) - 127.0), 8, axis=1)[..., None]
    return vals.transpose(0, 1, 3, 2).reshape(g * 512, n)


def sigmoid(v):
    return 1.0 / (1.0 + np.exp(-np.maximum(v, -700.0)))


K, T, S, N, H, U = 512, 2048, 512, 128, 512, 1024


def setup_inputs():
    n = np.random.standard_normal
    s = mx_kscale(K)[:, None]
    u = mx_kscale(H)
    packed_xT = pack_weight(n((K, T)) * s)
    return {
        "x_words": packed_xT[0],
        "x_scales": packed_xT[1],
        "w1": (n((K, H)) / np.sqrt(K) / s).astype(np.float32),
        "w2": (n((K, H)) / np.sqrt(K) / s).astype(np.float32),
        "page": (n((H, U))).astype(np.float32),
        "unit": (np.random.uniform(0.6, 1.4, (H, 1)) * u[:, None]).astype(np.float32),
        "w3": (n((H, N)) / np.sqrt(H) / u[:, None]).astype(np.float32),
        "offs": striped(np.random.permutation(T)[:S]),
        "at": striped(np.random.permutation(U)[:S]),
        "cop": striped(np.random.permutation(S)),
        "rd": striped(np.random.permutation(U)),
    }


def reference(x_words, x_scales, w1, w2, page, unit, w3, offs, at, cop, rd):
    xq = unpack_weight(x_words, x_scales)[:, unstriped(offs)]
    yg = mxq(f64(w2), 0, "e4m3").T @ xq
    fg = sigmoid(yg)
    old = f64(page)[:, unstriped(at)]
    y = mxq(f64(w1), 0, "e4m3").T @ xq
    neww = fg * old + (-1.0 * fg + 1.0) * np.tanh(y)
    ncp = neww[:, unstriped(cop)]
    wr = neww + 0.5 * ncp
    pnew = f64(page).copy()
    pnew[:, unstriped(at)] = wr
    read = pnew[:, unstriped(rd)]
    hid = f64(unit) * read
    return mxq(f64(w3), 0, "e4m3").T @ mxq(hid, 0, "e4m3")

@@ -1,0 +1,197 @@
+from contextlib import ExitStack
+
+import concourse.mybir as mybir
+
+K, T, S, N, H, U = 512, 2048, 512, 128, 512, 1024
+FLOPS = 2 * K * H * S * 2 + 2 * H * N * U
+
+F32 = mybir.dt.float32
+BF16 = mybir.dt.bfloat16
+I32 = mybir.dt.int32
+U32 = mybir.dt.uint32
+U16 = mybir.dt.uint16
+U8 = mybir.dt.uint8
+FP8X4 = mybir.dt.float8_e4m3fn_x4
+ALU = mybir.AluOpType
+ACT = mybir.ActivationFunctionType
+
+P = 128
+PACK = 4
+HALF = S // 2
+QUARTER = U // 4
+OLD_ON_SCALAR = 3
+
+
+def tile_picked_yrwpage_read_p_kernel(
+    tc, x_words, x_scales, w1, w2, page, unit, w3, offs, at, cop, rd, out
+):
+    nc = tc.nc
+    with ExitStack() as ctx:
+        keep = ctx.enter_context(tc.tile_pool(name="keep", bufs=1))
+        psum = ctx.enter_context(tc.psum_pool(name="psum", bufs=1))
+
+        def load_list(src, count, name):
+            tile = keep.tile([P, count // 16], U16, name=name)
+            nc.sync.dma_start(tile[:], src)
+            return tile
+
+        def entries(tile, first, count):
+            return tile[:, first // 16 : (first + count) // 16]
+
+        def load_rows(w, h, name):
+            raw = keep.tile([P, 2, H], F32, name=f"{name}_raw{h}")
+            nc.sync.dma_start(raw[:], w.rearrange("(p j) c -> p j c", j=PACK)[:, 2 * h : 2 * h + 2, :])
+            return raw
+
+        xs = keep.tile([P, T], U8, name="xs", align_bytes=64)
+        nc.vector.memset(xs[:].bitcast(I32), 0)
+        w1_raw = [load_rows(w1, 0, "w1")]
+        offs_t = load_list(offs, S, "offs_t")
+        for q in range(4):
+            nc.sync.dma_start(xs[32 * q : 32 * q + 4, :].bitcast(I32), x_scales[0, 4 * q : 4 * q + 4, :].bitcast(I32))
+        w1_raw.append(load_rows(w1, 1, "w1"))
+        xw = keep.tile([P, T], U32, name="xw", align_bytes=64)
+        nc.sync.dma_start(xw[:].bitcast(I32), x_words[0].rearrange("p n r -> p (n r)").bitcast(I32))
+        w2_raw = [load_rows(w2, h, "w2") for h in range(2)]
+        at_t = load_list(at, S, "at_t")
+        page_rows = page.rearrange("(p t) c -> t p c", t=PACK)
+        pages = []
+        for t in range(PACK):
+            page_t = keep.tile([P, U], F32, name=f"page{t}")
+            nc.sync.dma_start(page_t[:], page_rows[t])
+            pages.append(page_t)
+            if t == 1:
+                cop_t = load_list(cop, S, "cop_t")
+        w3_raw = keep.tile([P, PACK, N], F32, name="w3_raw")
+        nc.sync.dma_start(w3_raw[:], w3.rearrange("(p j) n -> p j n", j=PACK))
+        unit_t = keep.tile([P, PACK], F32, name="unit_t")
+        nc.sync.dma_start(unit_t[:], unit.rearrange("(p t) o -> p (t o)", t=PACK))
+        rd_t = load_list(rd, U, "rd_t")
+
+        def quantise_weight(raw_parts, name):
+            grouped = keep.tile([P, H * PACK], BF16, name=f"{name}_grouped", align_bytes=64)
+            dealt = grouped[:].rearrange("p (t m j) -> p m j t", t=PACK, j=PACK)
+            for h, raw in enumerate(raw_parts):
+                nc.vector.tensor_copy(dealt[:, :, 2 * h : 2 * h + 2, :], raw[:].rearrange("p j (m t) -> p m j t", t=PACK))
+            operands = []
+            for t in range(PACK):
+                codes = keep.tile([P, P], U32, name=f"{name}_codes{t}", align_bytes=64)
+                scales = keep.tile([P, P], U8, name=f"{name}_scales{t}", align_bytes=64)
+                nc.vector.quantize_mx(out=codes[:].bitcast(FP8X4), scales=scales[:], in_=grouped[:, t * H : (t + 1) * H])
+                operands.append((codes, scales))
+            return operands
+
+        def multiply(operands, name):
+            banks = []
+            for t, (codes, scales) in enumerate(operands):
+                bank = psum.tile([P, S], F32, name=f"{name}_bank{t}", tag=f"{name}_bank{t}")
+                nc.tensor.matmul_mx(
+                    out=bank[:], lhsT=codes[:].bitcast(FP8X4), lhsT_scale=scales[:],
+                    rhs=xq_words[:].bitcast(FP8X4), rhs_scale=xq_scales[:], start=True, stop=True,
+                )
+                banks.append(bank)
+            return banks
+
+        w1_q = quantise_weight(w1_raw, "w1")
+        xq_scales = keep.tile([P, S], U8, name="xq_scales", align_bytes=64)
+        nc.vector.tensor_copy(xq_scales[:], xs[:].indirect(offs_t[:]))
+        xq_words = keep.tile([P, S], U32, name="xq_words", align_bytes=64)
+        nc.vector.tensor_copy(xq_words[:], xw[:].indirect(offs_t[:]))
+        y_banks = multiply(w1_q, "w1")
+        yg_banks = multiply(quantise_weight(w2_raw, "w2"), "w2")
+
+        def activate(bank, scale, name):
+            result = keep.tile([P, S], F32, name=name)
+            nc.scalar.activation(result[:], bank[:], ACT.Tanh, scale=scale)
+            return result
+
+        cand, forget, old = [], [], []
+        for t in range(PACK):
+            cand.append(activate(y_banks[t], 1.0, f"cand{t}"))
+            if t < OLD_ON_SCALAR:
+                old_t = keep.tile([P, S], F32, name=f"old{t}")
+                nc.scalar.activation(old_t[:], pages[t][:].indirect(at_t[:]), ACT.Copy)
+                old.append(old_t[:])
+            else:
+                old.append(pages[t][:].indirect(at_t[:]))
+            forget.append(activate(yg_banks[t], 0.5, f"forget{t}"))
+
+        def differ(t):
+            diff = keep.tile([P, S], F32, name=f"diff{t}", tag="diff")
+            nc.vector.tensor_tensor(diff[:], old[t], cand[t][:], ALU.subtract)
+            return diff
+
+        def weigh(t, diff):
+            kept = keep.tile([P, S], F32, name=f"kept{t}", tag="kept")
+            nc.vector.scalar_tensor_tensor(kept[:], forget[t][:], 1.0, diff[:], ALU.add, ALU.mult)
+            return kept
+
+        def renew(t, kept):
+            neww = keep.tile([P, S], F32, name=f"neww{t}")
+            nc.vector.scalar_tensor_tensor(neww[:], kept[:], 0.5, cand[t][:], ALU.mult, ALU.add)
+            return neww
+
+        def halve(t, neww):
+            halved = keep.tile([P, S], F32, name=f"halved{t}", tag="halved", align_bytes=64)
+            nc.vector.tensor_scalar(halved[:], neww[:], 0.5, None, ALU.mult)
+            return halved
+
+        def write(t, neww, halved):
+            for s0 in (0, HALF):
+                wr = keep.tile([P, HALF], F32, name=f"wr{t}_{s0}")
+                nc.vector.tensor_tensor(wr[:], halved[:].indirect(entries(cop_t, s0, HALF)), neww[:, s0 : s0 + HALF], ALU.add)
+                nc.scalar.activation(pages[t][:].indirect(entries(at_t, s0, HALF)), wr[:], ACT.Copy)
+
+        neww = renew(0, weigh(0, differ(0)))
+        for t in range(1, PACK):
+            diff = differ(t)
+            halved = halve(t - 1, neww)
+            kept = weigh(t, diff)
+            write(t - 1, neww, halved)
+            neww = renew(t, kept)
+        w3_grouped = keep.tile([P, N, PACK], BF16, name="w3_grouped", align_bytes=64)
+        nc.vector.tensor_copy(w3_grouped[:], w3_raw[:].rearrange("p j n -> p n j"))
+        halved = halve(PACK - 1, neww)
+        w3_codes = keep.tile([P, N], U32, name="w3_codes", align_bytes=64)
+        w3_scales = keep.tile([P, N], U8, name="w3_scales", align_bytes=64)
+        nc.vector.quantize_mx(out=w3_codes[:].bitcast(FP8X4), scales=w3_scales[:], in_=w3_grouped[:].rearrange("p n j -> p (n j)"))
+        write(PACK - 1, neww, halved)
+
+        planes = keep.tile([P, PACK, U], BF16, name="planes", tag="halved", align_bytes=64)
+        for t in range(PACK - 1):
+            nc.vector.tensor_scalar(planes[:, t, :], pages[t][:], unit_t[:, t : t + 1], None, ALU.mult)
+        last = PACK - 1
+        split = U - QUARTER
+        nc.scalar.activation(planes[:, last, split:], pages[last][:, split:], ACT.Copy, scale=unit_t[:, last : last + 1])
+        nc.vector.tensor_scalar(planes[:, last, :split], pages[last][:, :split], unit_t[:, last : last + 1], None, ALU.mult)
+
+        product = keep.tile([P, U], F32, name="product")
+        for q in range(4):
+            cols = slice(q * QUARTER, (q + 1) * QUARTER)
+            hid = keep.tile([P, QUARTER * PACK], BF16, name=f"hid{q}", align_bytes=64)
+            woven = hid[:].rearrange("p (c i t) -> p c t i", i=4, t=PACK)
+            source = planes[:, :, cols].rearrange("p t (c i) -> p c t i", i=4)
+            if q == 3:
+                nc.scalar.copy(woven, source)
+            else:
+                nc.vector.tensor_copy(woven, source)
+            codes = keep.tile([P, QUARTER], U32, name=f"hid_codes{q}", align_bytes=64)
+            scales = keep.tile([P, QUARTER], U8, name=f"hid_scales{q}", align_bytes=64)
+            nc.vector.quantize_mx(out=codes[:].bitcast(FP8X4), scales=scales[:], in_=hid[:])
+            bank = psum.tile([P, QUARTER], F32, name=f"out_bank{q}", tag=f"w2_bank{q}")
+            nc.tensor.matmul_mx(
+                out=bank[:], lhsT=w3_codes[:].bitcast(FP8X4), lhsT_scale=w3_scales[:],
+                rhs=codes[:].bitcast(FP8X4), rhs_scale=scales[:], start=True, stop=True,
+            )
+            nc.scalar.copy(product[:, cols], bank[:])
+
+        for q in range(4):
+            cols = slice(q * QUARTER, (q + 1) * QUARTER)
+            picked = keep.tile([P, QUARTER], F32, name=f"picked{q}")
+            looked_up = product[:].indirect(entries(rd_t, q * QUARTER, QUARTER))
+            if q % 2 == 0:
+                nc.vector.tensor_copy(picked[:], looked_up)
+                nc.sync.dma_start(out[:, cols], picked[:])
+            else:
+                nc.scalar.activation(picked[:], looked_up, ACT.Copy)
+                nc.scalar.dma_start(out[:, cols], picked[:])

@@ -62,68 +62,62 @@ def tile_picked_yrwpage_read_p_kernel(
             pages.append(page_t)
             if t == 1:
                 cop_t = load_list(cop, S, "cop_t")
-        w3_raw = keep.tile([P, PACK, N], F32, name="w3_raw")
-        nc.sync.dma_start(w3_raw[:], w3.rearrange("(p j) n -> p j n", j=PACK))
+                w3_raw = keep.tile([P, PACK, N], F32, name="w3_raw")
+                nc.sync.dma_start(w3_raw[:], w3.rearrange("(p j) n -> p j n", j=PACK))
         unit_t = keep.tile([P, PACK], F32, name="unit_t")
         nc.sync.dma_start(unit_t[:], unit.rearrange("(p t) o -> p (t o)", t=PACK))
         rd_t = load_list(rd, U, "rd_t")
 
-        def quantise_weight(raw_parts, name):
+        def deal_weight(raw_parts, name):
             grouped = keep.tile([P, H * PACK], BF16, name=f"{name}_grouped", align_bytes=64)
             dealt = grouped[:].rearrange("p (t m j) -> p m j t", t=PACK, j=PACK)
             for h, raw in enumerate(raw_parts):
                 nc.vector.tensor_copy(dealt[:, :, 2 * h : 2 * h + 2, :], raw[:].rearrange("p j (m t) -> p m j t", t=PACK))
-            operands = []
-            for t in range(PACK):
-                codes = keep.tile([P, P], U32, name=f"{name}_codes{t}", align_bytes=64)
-                scales = keep.tile([P, P], U8, name=f"{name}_scales{t}", align_bytes=64)
-                nc.vector.quantize_mx(out=codes[:].bitcast(FP8X4), scales=scales[:], in_=grouped[:, t * H : (t + 1) * H])
-                operands.append((codes, scales))
-            return operands
+            return grouped
 
-        def multiply(operands, name):
-            banks = []
-            for t, (codes, scales) in enumerate(operands):
-                bank = psum.tile([P, S], F32, name=f"{name}_bank{t}", tag=f"{name}_bank{t}")
-                nc.tensor.matmul_mx(
-                    out=bank[:], lhsT=codes[:].bitcast(FP8X4), lhsT_scale=scales[:],
-                    rhs=xq_words[:].bitcast(FP8X4), rhs_scale=xq_scales[:], start=True, stop=True,
-                )
-                banks.append(bank)
-            return banks
+        def quantise(values, name):
+            width = values.shape[1] // PACK
+            codes = keep.tile([P, width], U32, name=f"{name}_codes", align_bytes=64)
+            scales = keep.tile([P, width], U8, name=f"{name}_scales", align_bytes=64)
+            nc.vector.quantize_mx(out=codes[:].bitcast(FP8X4), scales=scales[:], in_=values)
+            return codes[:], scales[:]
 
-        w1_q = quantise_weight(w1_raw, "w1")
+        def multiply(bank, stationary, moving):
+            nc.tensor.matmul_mx(
+                out=bank, lhsT=stationary[0].bitcast(FP8X4), lhsT_scale=stationary[1],
+                rhs=moving[0].bitcast(FP8X4), rhs_scale=moving[1], start=True, stop=True,
+            )
+
+        def tanh_of_product(stationary, scale, name):
+            bank = psum.tile([P, S], F32, name=f"{name}_bank", tag=f"{name}_bank")
+            multiply(bank[:], stationary, picked_x)
+            result = keep.tile([P, S], F32, name=name, tag=name, align_bytes=64)
+            nc.scalar.activation(result[:], bank[:], ACT.Tanh, scale=scale)
+            return result
+
+        w1_codes, w1_scales = quantise(deal_weight(w1_raw, "w1")[:], "w1")
         xq_scales = keep.tile([P, S], U8, name="xq_scales", align_bytes=64)
         nc.vector.tensor_copy(xq_scales[:], xs[:].indirect(offs_t[:]))
         xq_words = keep.tile([P, S], U32, name="xq_words", align_bytes=64)
         nc.vector.tensor_copy(xq_words[:], xw[:].indirect(offs_t[:]))
-        y_banks = multiply(w1_q, "w1")
-        yg_banks = multiply(quantise_weight(w2_raw, "w2"), "w2")
+        picked_x = (xq_words[:], xq_scales[:])
+        cand = [
+            tanh_of_product((w1_codes[:, t * P : (t + 1) * P], w1_scales[:, t * P : (t + 1) * P]), 1.0, f"cand{t}")
+            for t in range(PACK)
+        ]
+        w2_grouped = deal_weight(w2_raw, "w2")
 
-        def activate(bank, scale, name):
-            result = keep.tile([P, S], F32, name=name)
-            nc.scalar.activation(result[:], bank[:], ACT.Tanh, scale=scale)
-            return result
+        def gate(t):
+            return tanh_of_product(quantise(w2_grouped[:, t * H : (t + 1) * H], f"w2_{t}"), 0.5, f"gate{t}")
 
-        cand, forget, old = [], [], []
-        for t in range(PACK):
-            cand.append(activate(y_banks[t], 1.0, f"cand{t}"))
-            if t < OLD_ON_SCALAR:
-                old_t = keep.tile([P, S], F32, name=f"old{t}")
-                nc.scalar.activation(old_t[:], pages[t][:].indirect(at_t[:]), ACT.Copy)
-                old.append(old_t[:])
-            else:
-                old.append(pages[t][:].indirect(at_t[:]))
-            forget.append(activate(yg_banks[t], 0.5, f"forget{t}"))
-
-        def differ(t):
-            diff = keep.tile([P, S], F32, name=f"diff{t}", tag="diff")
-            nc.vector.tensor_tensor(diff[:], old[t], cand[t][:], ALU.subtract)
+        def differ(t, slot):
+            diff = keep.tile([P, S], F32, name=f"diff{t}", tag=slot)
+            nc.vector.tensor_tensor(diff[:], pages[t][:].indirect(at_t[:]), cand[t][:], ALU.subtract)
             return diff
 
         def weigh(t, diff):
-            kept = keep.tile([P, S], F32, name=f"kept{t}", tag="kept")
-            nc.vector.scalar_tensor_tensor(kept[:], forget[t][:], 1.0, diff[:], ALU.add, ALU.mult)
+            kept = keep.tile([P, S], F32, name=f"kept{t}", tag=f"kept{t}", align_bytes=64)
+            nc.vector.scalar_tensor_tensor(kept[:], gates[t][:], 1.0, diff[:], ALU.add, ALU.mult)
             return kept
 
         def renew(t, kept):
@@ -131,59 +125,86 @@ def tile_picked_yrwpage_read_p_kernel(
             nc.vector.scalar_tensor_tensor(neww[:], kept[:], 0.5, cand[t][:], ALU.mult, ALU.add)
             return neww
 
-        def halve(t, neww):
-            halved = keep.tile([P, S], F32, name=f"halved{t}", tag="halved", align_bytes=64)
-            nc.vector.tensor_scalar(halved[:], neww[:], 0.5, None, ALU.mult)
-            return halved
+        def fetch(neww, s0, target):
+            nc.scalar.activation(target, neww[:].indirect(entries(cop_t, s0, HALF)), ACT.Copy, scale=0.5)
+            return target
 
-        def write(t, neww, halved):
-            for s0 in (0, HALF):
-                wr = keep.tile([P, HALF], F32, name=f"wr{t}_{s0}")
-                nc.vector.tensor_tensor(wr[:], halved[:].indirect(entries(cop_t, s0, HALF)), neww[:, s0 : s0 + HALF], ALU.add)
-                nc.scalar.activation(pages[t][:].indirect(entries(at_t, s0, HALF)), wr[:], ACT.Copy)
+        def fetch_halves(t, neww):
+            return [fetch(neww, s0, keep.tile([P, HALF], F32, name=f"ncp{t}_{s0}", tag=f"ncp{t}_{s0}")[:]) for s0 in (0, HALF)]
 
-        neww = renew(0, weigh(0, differ(0)))
-        for t in range(1, PACK):
-            diff = differ(t)
-            halved = halve(t - 1, neww)
-            kept = weigh(t, diff)
-            write(t - 1, neww, halved)
-            neww = renew(t, kept)
+        def write_back(t, wr, s0):
+            nc.scalar.activation(pages[t][:].indirect(entries(at_t, s0, HALF)), wr, ACT.Copy)
+
+        def add_and_write(t, neww, ncp, h, slot):
+            s0 = h * HALF
+            wr = keep.tile([P, HALF], F32, name=f"wr{t}_{h}", tag=slot, align_bytes=64)
+            nc.vector.tensor_tensor(wr[:], ncp[h], neww[:, s0 : s0 + HALF], ALU.add)
+            write_back(t, wr[:], s0)
+
+        gates = [gate(t) for t in range(PACK - 1)]
+        diff0 = differ(0, "diff")
+        gates.append(gate(PACK - 1))
+        kept0 = weigh(0, diff0)
         w3_grouped = keep.tile([P, N, PACK], BF16, name="w3_grouped", align_bytes=64)
         nc.vector.tensor_copy(w3_grouped[:], w3_raw[:].rearrange("p j n -> p n j"))
-        halved = halve(PACK - 1, neww)
-        w3_codes = keep.tile([P, N], U32, name="w3_codes", align_bytes=64)
-        w3_scales = keep.tile([P, N], U8, name="w3_scales", align_bytes=64)
-        nc.vector.quantize_mx(out=w3_codes[:].bitcast(FP8X4), scales=w3_scales[:], in_=w3_grouped[:].rearrange("p n j -> p (n j)"))
-        write(PACK - 1, neww, halved)
+        neww0 = renew(0, kept0)
+        ncp0 = fetch_halves(0, neww0)
+        diff1 = differ(1, "diff")
+        add_and_write(0, neww0, ncp0, 0, "wr0_0")
+        kept1 = weigh(1, diff1)
+        w3_q = quantise(w3_grouped[:].rearrange("p n j -> p (n j)"), "w3")
+        neww1 = renew(1, kept1)
+        ncp1 = fetch_halves(1, neww1)
+        diff2 = differ(2, "diff")
+        add_and_write(0, neww0, ncp0, 1, "kept1")
+        kept2 = weigh(2, diff2)
+        add_and_write(1, neww1, ncp1, 0, "gate2")
+        neww2 = renew(2, kept2)
+        diff3 = differ(3, "diff")
+        add_and_write(1, neww1, ncp1, 1, "kept2")
+        kept3 = weigh(3, diff3)
+        halved2 = keep.tile([P, S], F32, name="halved2")
+        nc.vector.tensor_scalar(halved2[:], neww2[:], 0.5, None, ALU.mult)
+        neww3 = renew(3, kept3)
 
-        planes = keep.tile([P, PACK, U], BF16, name="planes", tag="halved", align_bytes=64)
-        for t in range(PACK - 1):
-            nc.vector.tensor_scalar(planes[:, t, :], pages[t][:], unit_t[:, t : t + 1], None, ALU.mult)
-        last = PACK - 1
-        split = U - QUARTER
-        nc.scalar.activation(planes[:, last, split:], pages[last][:, split:], ACT.Copy, scale=unit_t[:, last : last + 1])
-        nc.vector.tensor_scalar(planes[:, last, :split], pages[last][:, :split], unit_t[:, last : last + 1], None, ALU.mult)
+        planes = keep.tile([P, PACK, U], BF16, name="planes", tag="kept3", align_bytes=64)
+        front, back = slice(0, U // 2), slice(U // 2, U)
 
-        product = keep.tile([P, U], F32, name="product")
-        for q in range(4):
+        def scale_on_vector(t, cols):
+            nc.vector.tensor_scalar(planes[:, t, cols], pages[t][:, cols], unit_t[:, t : t + 1], None, ALU.mult)
+
+        ncp3 = [fetch(neww3, h * HALF, planes[:, 1, cols].bitcast(F32)) for h, cols in enumerate((front, back))]
+        wr2 = keep.tile([P, S], F32, name="wr2", tag="cand3", align_bytes=64)
+
+        def fetch_add_and_write(s0):
+            cols = slice(s0, s0 + HALF)
+            nc.vector.tensor_tensor(wr2[:, cols], halved2[:].indirect(entries(cop_t, s0, HALF)), neww2[:, cols], ALU.add)
+            write_back(2, wr2[:, cols], s0)
+
+        fetch_add_and_write(0)
+        scale_on_vector(0, slice(0, U))
+        fetch_add_and_write(HALF)
+        for h in range(2):
+            s0 = h * HALF
+            nc.vector.tensor_tensor(pages[3][:].indirect(entries(at_t, s0, HALF)), ncp3[h], neww3[:, s0 : s0 + HALF], ALU.add)
+        for cols in (back, front):
+            scale_on_vector(1, cols)
+            scale_on_vector(3, cols)
+            nc.scalar.activation(planes[:, 2, cols], pages[2][:, cols], ACT.Copy, scale=unit_t[:, 2:3])
+
+        def weave(q, copy):
             cols = slice(q * QUARTER, (q + 1) * QUARTER)
             hid = keep.tile([P, QUARTER * PACK], BF16, name=f"hid{q}", align_bytes=64)
-            woven = hid[:].rearrange("p (c i t) -> p c t i", i=4, t=PACK)
-            source = planes[:, :, cols].rearrange("p t (c i) -> p c t i", i=4)
-            if q == 3:
-                nc.scalar.copy(woven, source)
-            else:
-                nc.vector.tensor_copy(woven, source)
-            codes = keep.tile([P, QUARTER], U32, name=f"hid_codes{q}", align_bytes=64)
-            scales = keep.tile([P, QUARTER], U8, name=f"hid_scales{q}", align_bytes=64)
-            nc.vector.quantize_mx(out=codes[:].bitcast(FP8X4), scales=scales[:], in_=hid[:])
-            bank = psum.tile([P, QUARTER], F32, name=f"out_bank{q}", tag=f"w2_bank{q}")
-            nc.tensor.matmul_mx(
-                out=bank[:], lhsT=w3_codes[:].bitcast(FP8X4), lhsT_scale=w3_scales[:],
-                rhs=codes[:].bitcast(FP8X4), rhs_scale=scales[:], start=True, stop=True,
-            )
-            nc.scalar.copy(product[:, cols], bank[:])
+            copy(hid[:].rearrange("p (c i t) -> p c t i", i=4, t=PACK), planes[:, :, cols].rearrange("p t (c i) -> p c t i", i=4))
+            return hid
+
+        product = keep.tile([P, U], F32, name="product")
+        hids = [weave(q, nc.vector.tensor_copy if q < 2 else nc.scalar.copy) for q in range(4)]
+        for q in range(4):
+            bank = psum.tile([P, QUARTER], F32, name=f"out_bank{q}", tag=f"cand{q}_bank")
+            multiply(bank[:], w3_q, quantise(hids[q][:], f"hid{q}"))
+            copy = nc.vector.tensor_copy if q == 3 else nc.scalar.copy
+            copy(product[:, q * QUARTER : (q + 1) * QUARTER], bank[:])
 
         for q in range(4):
             cols = slice(q * QUARTER, (q + 1) * QUARTER)

@@ -45,11 +45,13 @@ def tile_picked_yrwpage_read_p_kernel(
 
         xs = keep.tile([P, T], U8, name="xs", align_bytes=64)
         nc.vector.memset(xs[:].bitcast(I32), 0)
-        w1_raw = [load_rows(w1, 0, "w1")]
+        w1_rows = w1.rearrange("(p j) c -> p j c", j=PACK)
+        w1_raw = keep.tile([P, PACK, H], F32, name="w1_raw")
+        nc.sync.dma_start(w1_raw[:, :2, :], w1_rows[:, :2, :])
         offs_t = load_list(offs, S, "offs_t")
         for q in range(4):
             nc.sync.dma_start(xs[32 * q : 32 * q + 4, :].bitcast(I32), x_scales[0, 4 * q : 4 * q + 4, :].bitcast(I32))
-        w1_raw.append(load_rows(w1, 1, "w1"))
+        nc.sync.dma_start(w1_raw[:, 2:, :], w1_rows[:, 2:, :])
         xw = keep.tile([P, T], U32, name="xw", align_bytes=64)
         nc.sync.dma_start(xw[:].bitcast(I32), x_words[0].rearrange("p n r -> p (n r)").bitcast(I32))
         w2_raw = [load_rows(w2, h, "w2") for h in range(2)]
@@ -95,7 +97,11 @@ def tile_picked_yrwpage_read_p_kernel(
             nc.scalar.activation(result[:], bank[:], ACT.Tanh, scale=scale)
             return result
 
-        w1_codes, w1_scales = quantise(deal_weight(w1_raw, "w1")[:], "w1")
+        w1_grouped = keep.tile([P, H * PACK], BF16, name="w1_grouped", align_bytes=64)
+        nc.vector.tensor_copy(
+            w1_grouped[:].rearrange("p (t m j) -> p m j t", t=PACK, j=PACK), w1_raw[:].rearrange("p j (m t) -> p m j t", t=PACK)
+        )
+        w1_codes, w1_scales = quantise(w1_grouped[:], "w1")
         xq_scales = keep.tile([P, S], U8, name="xq_scales", align_bytes=64)
         nc.vector.tensor_copy(xq_scales[:], xs[:].indirect(offs_t[:]))
         xq_words = keep.tile([P, S], U32, name="xq_words", align_bytes=64)
@@ -167,13 +173,15 @@ def tile_picked_yrwpage_read_p_kernel(
         nc.vector.tensor_scalar(halved2[:], neww2[:], 0.5, None, ALU.mult)
         neww3 = renew(3, kept3)
 
-        planes = keep.tile([P, PACK, U], BF16, name="planes", tag="kept3", align_bytes=64)
+        planes = keep.tile([P, PACK, U], BF16, name="planes", tag="gate3", align_bytes=64)
         front, back = slice(0, U // 2), slice(U // 2, U)
 
         def scale_on_vector(t, cols):
             nc.vector.tensor_scalar(planes[:, t, cols], pages[t][:, cols], unit_t[:, t : t + 1], None, ALU.mult)
 
-        ncp3 = [fetch(neww3, h * HALF, planes[:, 1, cols].bitcast(F32)) for h, cols in enumerate((front, back))]
+        ncp3 = planes[:, 1, :].bitcast(F32)
+        for s0 in (0, HALF):
+            fetch(neww3, s0, ncp3[:, s0 : s0 + HALF])
         wr2 = keep.tile([P, S], F32, name="wr2", tag="cand3", align_bytes=64)
 
         def fetch_add_and_write(s0):
@@ -181,12 +189,10 @@ def tile_picked_yrwpage_read_p_kernel(
             nc.vector.tensor_tensor(wr2[:, cols], halved2[:].indirect(entries(cop_t, s0, HALF)), neww2[:, cols], ALU.add)
             write_back(2, wr2[:, cols], s0)
 
-        fetch_add_and_write(0)
         scale_on_vector(0, slice(0, U))
+        fetch_add_and_write(0)
         fetch_add_and_write(HALF)
-        for h in range(2):
-            s0 = h * HALF
-            nc.vector.tensor_tensor(pages[3][:].indirect(entries(at_t, s0, HALF)), ncp3[h], neww3[:, s0 : s0 + HALF], ALU.add)
+        nc.vector.tensor_tensor(pages[3][:].indirect(at_t[:]), ncp3, neww3[:], ALU.add)
         for cols in (back, front):
             scale_on_vector(1, cols)
             scale_on_vector(3, cols)

from contextlib import ExitStack

import concourse.mybir as mybir

K, T, S, N, H, U = 512, 2048, 512, 128, 512, 1024
FLOPS = 2 * K * H * S * 2 + 2 * H * N * U

F32 = mybir.dt.float32
BF16 = mybir.dt.bfloat16
I32 = mybir.dt.int32
U32 = mybir.dt.uint32
U16 = mybir.dt.uint16
U8 = mybir.dt.uint8
FP8X4 = mybir.dt.float8_e4m3fn_x4
ALU = mybir.AluOpType
ACT = mybir.ActivationFunctionType

P = 128
PACK = 4
HALF = S // 2
QUARTER = U // 4
OLD_ON_SCALAR = 3


def tile_picked_yrwpage_read_p_kernel(
    tc, x_words, x_scales, w1, w2, page, unit, w3, offs, at, cop, rd, out
):
    nc = tc.nc
    with ExitStack() as ctx:
        keep = ctx.enter_context(tc.tile_pool(name="keep", bufs=1))
        psum = ctx.enter_context(tc.psum_pool(name="psum", bufs=1))

        def load_list(src, count, name):
            tile = keep.tile([P, count // 16], U16, name=name)
            nc.sync.dma_start(tile[:], src)
            return tile

        def entries(tile, first, count):
            return tile[:, first // 16 : (first + count) // 16]

        def load_rows(w, h, name):
            raw = keep.tile([P, 2, H], F32, name=f"{name}_raw{h}")
            nc.sync.dma_start(raw[:], w.rearrange("(p j) c -> p j c", j=PACK)[:, 2 * h : 2 * h + 2, :])
            return raw

        xs = keep.tile([P, T], U8, name="xs", align_bytes=64)
        nc.vector.memset(xs[:].bitcast(I32), 0)
        w1_rows = w1.rearrange("(p j) c -> p j c", j=PACK)
        w1_raw = keep.tile([P, PACK, H], F32, name="w1_raw")
        nc.sync.dma_start(w1_raw[:, :2, :], w1_rows[:, :2, :])
        offs_t = load_list(offs, S, "offs_t")
        for q in range(4):
            nc.sync.dma_start(xs[32 * q : 32 * q + 4, :].bitcast(I32), x_scales[0, 4 * q : 4 * q + 4, :].bitcast(I32))
        nc.sync.dma_start(w1_raw[:, 2:, :], w1_rows[:, 2:, :])
        xw = keep.tile([P, T], U32, name="xw", align_bytes=64)
        nc.sync.dma_start(xw[:].bitcast(I32), x_words[0].rearrange("p n r -> p (n r)").bitcast(I32))
        w2_raw = [load_rows(w2, h, "w2") for h in range(2)]
        at_t = load_list(at, S, "at_t")
        page_rows = page.rearrange("(p t) c -> t p c", t=PACK)
        pages = []
        for t in range(PACK):
            page_t = keep.tile([P, U], F32, name=f"page{t}")
            nc.sync.dma_start(page_t[:], page_rows[t])
            pages.append(page_t)
            if t == 1:
                cop_t = load_list(cop, S, "cop_t")
                w3_raw = keep.tile([P, PACK, N], F32, name="w3_raw")
                nc.sync.dma_start(w3_raw[:], w3.rearrange("(p j) n -> p j n", j=PACK))
        unit_t = keep.tile([P, PACK], F32, name="unit_t")
        nc.sync.dma_start(unit_t[:], unit.rearrange("(p t) o -> p (t o)", t=PACK))
        rd_t = load_list(rd, U, "rd_t")

        def deal_weight(raw_parts, name):
            grouped = keep.tile([P, H * PACK], BF16, name=f"{name}_grouped", align_bytes=64)
            dealt = grouped[:].rearrange("p (t m j) -> p m j t", t=PACK, j=PACK)
            for h, raw in enumerate(raw_parts):
                nc.vector.tensor_copy(dealt[:, :, 2 * h : 2 * h + 2, :], raw[:].rearrange("p j (m t) -> p m j t", t=PACK))
            return grouped

        def quantise(values, name):
            width = values.shape[1] // PACK
            codes = keep.tile([P, width], U32, name=f"{name}_codes", align_bytes=64)
            scales = keep.tile([P, width], U8, name=f"{name}_scales", align_bytes=64)
            nc.vector.quantize_mx(out=codes[:].bitcast(FP8X4), scales=scales[:], in_=values)
            return codes[:], scales[:]

        def multiply(bank, stationary, moving):
            nc.tensor.matmul_mx(
                out=bank, lhsT=stationary[0].bitcast(FP8X4), lhsT_scale=stationary[1],
                rhs=moving[0].bitcast(FP8X4), rhs_scale=moving[1], start=True, stop=True,
            )

        def tanh_of_product(stationary, scale, name):
            bank = psum.tile([P, S], F32, name=f"{name}_bank", tag=f"{name}_bank")
            multiply(bank[:], stationary, picked_x)
            result = keep.tile([P, S], F32, name=name, tag=name, align_bytes=64)
            nc.scalar.activation(result[:], bank[:], ACT.Tanh, scale=scale)
            return result

        w1_grouped = keep.tile([P, H * PACK], BF16, name="w1_grouped", align_bytes=64)
        nc.vector.tensor_copy(
            w1_grouped[:].rearrange("p (t m j) -> p m j t", t=PACK, j=PACK), w1_raw[:].rearrange("p j (m t) -> p m j t", t=PACK)
        )
        w1_codes, w1_scales = quantise(w1_grouped[:], "w1")
        xq_scales = keep.tile([P, S], U8, name="xq_scales", align_bytes=64)
        nc.vector.tensor_copy(xq_scales[:], xs[:].indirect(offs_t[:]))
        xq_words = keep.tile([P, S], U32, name="xq_words", align_bytes=64)
        nc.vector.tensor_copy(xq_words[:], xw[:].indirect(offs_t[:]))
        picked_x = (xq_words[:], xq_scales[:])
        cand = [
            tanh_of_product((w1_codes[:, t * P : (t + 1) * P], w1_scales[:, t * P : (t + 1) * P]), 1.0, f"cand{t}")
            for t in range(PACK)
        ]
        w2_grouped = deal_weight(w2_raw, "w2")

        def gate(t):
            return tanh_of_product(quantise(w2_grouped[:, t * H : (t + 1) * H], f"w2_{t}"), 0.5, f"gate{t}")

        def differ(t, slot):
            diff = keep.tile([P, S], F32, name=f"diff{t}", tag=slot)
            nc.vector.tensor_tensor(diff[:], pages[t][:].indirect(at_t[:]), cand[t][:], ALU.subtract)
            return diff

        def weigh(t, diff):
            kept = keep.tile([P, S], F32, name=f"kept{t}", tag=f"kept{t}", align_bytes=64)
            nc.vector.scalar_tensor_tensor(kept[:], gates[t][:], 1.0, diff[:], ALU.add, ALU.mult)
            return kept

        def renew(t, kept):
            neww = keep.tile([P, S], F32, name=f"neww{t}")
            nc.vector.scalar_tensor_tensor(neww[:], kept[:], 0.5, cand[t][:], ALU.mult, ALU.add)
            return neww

        def fetch(neww, s0, target):
            nc.scalar.activation(target, neww[:].indirect(entries(cop_t, s0, HALF)), ACT.Copy, scale=0.5)
            return target

        def fetch_halves(t, neww):
            return [fetch(neww, s0, keep.tile([P, HALF], F32, name=f"ncp{t}_{s0}", tag=f"ncp{t}_{s0}")[:]) for s0 in (0, HALF)]

        def write_back(t, wr, s0):
            nc.scalar.activation(pages[t][:].indirect(entries(at_t, s0, HALF)), wr, ACT.Copy)

        def add_and_write(t, neww, ncp, h, slot):
            s0 = h * HALF
            wr = keep.tile([P, HALF], F32, name=f"wr{t}_{h}", tag=slot, align_bytes=64)
            nc.vector.tensor_tensor(wr[:], ncp[h], neww[:, s0 : s0 + HALF], ALU.add)
            write_back(t, wr[:], s0)

        gates = [gate(t) for t in range(PACK - 1)]
        diff0 = differ(0, "diff")
        gates.append(gate(PACK - 1))
        kept0 = weigh(0, diff0)
        w3_grouped = keep.tile([P, N, PACK], BF16, name="w3_grouped", align_bytes=64)
        nc.vector.tensor_copy(w3_grouped[:], w3_raw[:].rearrange("p j n -> p n j"))
        neww0 = renew(0, kept0)
        ncp0 = fetch_halves(0, neww0)
        diff1 = differ(1, "diff")
        add_and_write(0, neww0, ncp0, 0, "wr0_0")
        kept1 = weigh(1, diff1)
        w3_q = quantise(w3_grouped[:].rearrange("p n j -> p (n j)"), "w3")
        neww1 = renew(1, kept1)
        ncp1 = fetch_halves(1, neww1)
        diff2 = differ(2, "diff")
        add_and_write(0, neww0, ncp0, 1, "kept1")
        kept2 = weigh(2, diff2)
        add_and_write(1, neww1, ncp1, 0, "gate2")
        neww2 = renew(2, kept2)
        diff3 = differ(3, "diff")
        add_and_write(1, neww1, ncp1, 1, "kept2")
        kept3 = weigh(3, diff3)
        halved2 = keep.tile([P, S], F32, name="halved2")
        nc.vector.tensor_scalar(halved2[:], neww2[:], 0.5, None, ALU.mult)
        neww3 = renew(3, kept3)

        planes = keep.tile([P, PACK, U], BF16, name="planes", tag="gate3", align_bytes=64)
        front, back = slice(0, U // 2), slice(U // 2, U)

        def scale_on_vector(t, cols):
            nc.vector.tensor_scalar(planes[:, t, cols], pages[t][:, cols], unit_t[:, t : t + 1], None, ALU.mult)

        ncp3 = planes[:, 1, :].bitcast(F32)
        for s0 in (0, HALF):
            fetch(neww3, s0, ncp3[:, s0 : s0 + HALF])
        wr2 = keep.tile([P, S], F32, name="wr2", tag="cand3", align_bytes=64)

        def fetch_add_and_write(s0):
            cols = slice(s0, s0 + HALF)
            nc.vector.tensor_tensor(wr2[:, cols], halved2[:].indirect(entries(cop_t, s0, HALF)), neww2[:, cols], ALU.add)
            write_back(2, wr2[:, cols], s0)

        scale_on_vector(0, slice(0, U))
        fetch_add_and_write(0)
        fetch_add_and_write(HALF)
        nc.vector.tensor_tensor(pages[3][:].indirect(at_t[:]), ncp3, neww3[:], ALU.add)
        for cols in (back, front):
            scale_on_vector(1, cols)
            scale_on_vector(3, cols)
            nc.scalar.activation(planes[:, 2, cols], pages[2][:, cols], ACT.Copy, scale=unit_t[:, 2:3])

        def weave(q, copy):
            cols = slice(q * QUARTER, (q + 1) * QUARTER)
            hid = keep.tile([P, QUARTER * PACK], BF16, name=f"hid{q}", align_bytes=64)
            copy(hid[:].rearrange("p (c i t) -> p c t i", i=4, t=PACK), planes[:, :, cols].rearrange("p t (c i) -> p c t i", i=4))
            return hid

        product = keep.tile([P, U], F32, name="product")
        hids = [weave(q, nc.vector.tensor_copy if q < 2 else nc.scalar.copy) for q in range(4)]
        for q in range(4):
            bank = psum.tile([P, QUARTER], F32, name=f"out_bank{q}", tag=f"cand{q}_bank")
            multiply(bank[:], w3_q, quantise(hids[q][:], f"hid{q}"))
            copy = nc.vector.tensor_copy if q == 3 else nc.scalar.copy
            copy(product[:, q * QUARTER : (q + 1) * QUARTER], bank[:])

        for q in range(4):
            cols = slice(q * QUARTER, (q + 1) * QUARTER)
            picked = keep.tile([P, QUARTER], F32, name=f"picked{q}")
            looked_up = product[:].indirect(entries(rd_t, q * QUARTER, QUARTER))
            if q % 2 == 0:
                nc.vector.tensor_copy(picked[:], looked_up)
                nc.sync.dma_start(out[:, cols], picked[:])
            else:
                nc.scalar.activation(picked[:], looked_up, ACT.Copy)
                nc.scalar.dma_start(out[:, cols], picked[:])
